import numpy as np, ml_dtypes
CORES = [35,38,43,46]
N = 4
import mx_ref
BF = ml_dtypes.bfloat16
def entries(a):
    return np.ascontiguousarray(a.T).reshape(-1)
def table(e):
    return np.ascontiguousarray(np.reshape(e, (-1, 16)).T).astype(np.int32)
def cols(t, e):
    v = np.concatenate([t.reshape(128, -1, 4), np.zeros((128, 1, 4), BF)], axis=1)
    return np.ascontiguousarray(v[:, e]).reshape(128, -1)
def tile(rs):
    return np.stack(rs, axis=2).reshape(128, -1).astype(BF)
def cut(t, i, w=512):
    return t[:, w * i:w * i + w]
def f(rng, *shape):
    return mx_ref.flush((rng.standard_normal(shape, dtype=np.float32) * np.exp2(rng.integers(-2, 3, shape[:-1] + (1,)))).astype(BF))
def wide(rng, *shape, cols=0):
    v = rng.standard_normal(shape, dtype=np.float32) * np.exp2(rng.integers(-12, 13, shape)).astype(np.float32)
    if cols: v *= np.repeat(np.exp2(rng.integers(-cols, cols + 1, shape[:-2] + (1, shape[-1] // 4))) * (rng.random(shape[:-2] + (1, shape[-1] // 4)) > 0.0625), 4, axis=-1).astype(np.float32)
    return mx_ref.flush(v.astype(BF))
T, CAPA, CAPB, TR = 512, 160, 136, 40
def mix(rng, n, la=0, lb=0):
    n = n.copy()
    for _ in range(4000):
        p, q = rng.integers(0, N, (2, 3)); k = rng.integers(0, 4)
        p2, q2 = p.copy(), q.copy(); m = n.copy()
        if k == 3: p2[1] = q[1]
        else: p2[k], q2[k] = q[k], p[k]
        m[tuple(p)] -= 1; m[tuple(p2)] += 1
        if k < 3: m[tuple(q)] -= 1; m[tuple(q2)] += 1
        sa, ab = m.sum(axis=2), m.sum(axis=0)
        if m.min() >= 0 and m.max() <= TR and (sa <= CAPA).all() and (sa >= la).all() and (ab <= CAPB).all() and (ab >= lb).all(): n = m
    return n
def even():
    return np.full((N, N, N), T // N ** 2)
def places(rng, k, cap, by=None):
    out = np.zeros(len(k), int)
    for g in np.unique(k):
        j = np.flatnonzero(k == g)
        if by is None: out[j] = g * cap + rng.permutation(cap)[:len(j)]
        else: out[j[np.argsort(by[j])]] = g * cap + cap - 1 - np.arange(len(j))
    return out
def lists(rng, n, back=False):
    s, a, b = np.repeat(np.argwhere(n >= 0), n.reshape(-1), axis=0).T
    col = np.concatenate([rng.permutation(T) for r in range(N)])
    snd, pas, tri = np.full(N * N * CAPA, -1), np.full(N * N * CAPB, -1), np.full(N * N * N * TR, -1)
    p1 = places(rng, s * N + a, CAPA, col if back else None); snd[p1] = col
    arr = s * CAPA + p1 % CAPA
    p2 = places(rng, a * N + b, CAPB, arr if back else None); pas[p2] = arr
    p3 = places(rng, (s * N + a) * N + b, TR, col if back else None); tri[p3] = col
    c, t = a * CAPB + p2 % CAPB, (s * N + a) * TR + p3 % TR
    plc, plt = [], []
    for r in range(N):
        j = rng.permutation(np.flatnonzero(b == r))
        if back: j = j[np.argsort(-c[j])]
        plc.append(table(c[j])); plt.append(table(t[j]))
    return {"snd": np.stack([table(v) for v in snd.reshape(N, -1)]), "pas": np.stack([table(v) for v in pas.reshape(N, -1)]), "tri": np.stack([table(v) for v in tri.reshape(N, -1)]), "plc": np.stack(plc), "plt": np.stack(plt)}
def values(rng):
    return {"x": f(rng, N, 128, 4 * T), "w": f(rng, N, 128, 2048), "vv": f(rng, N, 128, 512)}
def setup_inputs(rng):
    return {**values(rng), **lists(rng, mix(rng, even()))}
def heavy(rng, d):
    n = even()
    for k in range(CAPB // N - T // N ** 2):
        for s in range(N):
            for a in range(N):
                n[s, a, (a + d) % N] += 1; n[s, a, (a + d + 1 + (s + k) % (N - 1)) % N] -= 1
    return {**values(rng), **lists(rng, mix(rng, n, lb=CAPB * np.roll(np.eye(N, dtype=int), d, axis=1)))}
def setup_inputs_diag(rng):
    return heavy(rng, 0)
def setup_inputs_onward(rng):
    return heavy(rng, int(rng.integers(1, N)))
def setup_inputs_full(rng):
    k = T // CAPA
    g = np.zeros((N, N), int); g[:, :k] = CAPA; g[:, k] = T - k * CAPA
    g = np.stack([np.roll(g[s], s) for s in range(N)])[rng.permutation(N)][:, rng.permutation(N)]
    return {**values(rng), **lists(rng, mix(rng, np.repeat(g[:, :, None] // N, N, axis=2), la=np.where(g == CAPA, CAPA, 0)))}
def setup_inputs_reversed(rng):
    return {**values(rng), **lists(rng, mix(rng, even()), back=True)}
def setup_inputs_spread(rng):
    d = setup_inputs(rng); d["x"] = wide(rng, N, 128, 4 * T); return d
def check_inputs(d):
    b = []
    snd, pas, tri, plc, plt = [[entries(d[k][r]) for r in range(N)] for k in ("snd", "pas", "tri", "plc", "plt")]
    for r in range(N):
        if snd[r].min() < -1 or not np.array_equal(np.sort(snd[r][snd[r] >= 0]), np.arange(T)): b.append("snd")
        if tri[r].min() < -1 or not np.array_equal(np.sort(tri[r][tri[r] >= 0]), np.arange(T)): b.append("tri")
        for a in range(N):
            u, v = snd[r][a * CAPA:(a + 1) * CAPA], tri[r][a * N * TR:(a + 1) * N * TR]
            if not np.array_equal(np.sort(u[u >= 0]), np.sort(v[v >= 0])): b.append("tri")
    arrived = [np.concatenate([snd[s][a * CAPA:(a + 1) * CAPA] for s in range(N)]) for a in range(N)]
    for a in range(N):
        if pas[a].min() < -1 or not np.array_equal(np.sort(pas[a][pas[a] >= 0]), np.flatnonzero(arrived[a] >= 0)): b.append("pas")
    if b: return b
    for r in range(N):
        k = np.concatenate([pas[a][r * CAPB:(r + 1) * CAPB] for a in range(N)])
        t = np.concatenate([tri[s][(a * N + r) * TR:(a * N + r + 1) * TR] for s in range(N) for a in range(N)])
        if not np.array_equal(np.sort(plc[r]), np.flatnonzero(k >= 0)): b.append("plc"); continue
        if not np.array_equal(np.sort(plt[r]), np.flatnonzero(t >= 0)): b.append("plt"); continue
        a, m = plc[r] // CAPB, k[plc[r]]
        if (plt[r] // TR != m // CAPA * N + a).any() or (t[plt[r]] != np.stack(arrived)[a, m]).any(): b.append("plt")
    return b
def reference(x, w, vv, snd, pas, tri, plc, plt):
    h = []
    for a in range(N):
        q = mx_ref.quantize(np.concatenate([cols(x[s], entries(snd[s])[a * CAPA:(a + 1) * CAPA]) for s in range(N)], axis=1))
        h.append(tile([np.maximum(mx_ref.matmul(mx_ref.quantize(cut(w[a], i)), q), np.float32(0)) * np.float32(0.043) for i in range(4)]))
    y = np.zeros((N, 128, T), np.float32)
    for b in range(N):
        t = np.concatenate([cols(h[a], entries(pas[a])[b * CAPB:(b + 1) * CAPB]) for a in range(N)], axis=1)
        y[b] = mx_ref.matmul(mx_ref.quantize(vv[b]), mx_ref.quantize(cols(t, entries(plc[b]))))
    return {"y": y}

@@ -1,0 +1,230 @@
+from concourse.bass import DstId, RemoteDMATransfer
+from concourse.mybir import dt, AluOpType, ActivationFunctionType
+
+N, TR = 4, 40
+C = N * TR
+W = N * C
+L = C // 16
+F8 = "float8_e4m3fn_x4"
+SCRATCH = {
+    "xb": ("sbuf", [128, 2048], "bfloat16"),
+    "wb": ("sbuf", [128, 2048], "bfloat16"),
+    "vb": ("sbuf", [128, 512], "bfloat16"),
+    "trl": ("sbuf", [128, 40], "int32"),
+    "plr": ("sbuf", [128, 32], "int32"),
+    "toff": ("sbuf", [128, 40], "uint16"),
+    "poff": ("sbuf", [128, 32], "uint16"),
+    "kf": ("sbuf", [128, 32], "float32"),
+    "ki": ("sbuf", [128, 32], "int32"),
+    "ks": ("sbuf", [128, 32], "int32"),
+    "ka": ("sbuf", [128, 32], "int32"),
+    "kd": ("sbuf", [128, 32], "int32"),
+    "ke": ("sbuf", [128, 32], "int32"),
+    "kp": ("sbuf", [128, 32], "int32"),
+    "xg": ("sbuf", [128, 4 * W], "bfloat16"),
+    "qx": ("sbuf", [128, W], F8),
+    "sx": ("sbuf", [128, W], "uint8"),
+    "rx": ("sbuf", [128, W], F8),
+    "rsx": ("sbuf", [128, W], "uint8"),
+    "wq": ("sbuf", [128, 512], F8),
+    "ws": ("sbuf", [128, 512], "uint8"),
+    "vq": ("sbuf", [128, 128], F8),
+    "vs": ("sbuf", [128, 128], "uint8"),
+    "h": ("sbuf", [128, N, 4 * C], "bfloat16"),
+    "qh": ("sbuf", [128, W], F8),
+    "sh": ("sbuf", [128, W], "uint8"),
+    "rh": ("sbuf", [128, W], F8),
+    "rsh": ("sbuf", [128, W], "uint8"),
+    "ps": ("psum", [128, 4096], "float32"),
+    "ysb": ("sbuf", [128, W], "float32"),
+    "yo": ("sbuf", [128, 512], "float32"),
+}
+SEMAPHORES = (["tl", "xl", "wl", "vl", "pl", "tof", "gf", "gn", "go", "qxf", "qxn", "qxo", "qw", "qv",
+               "rr", "qhf", "qhn", "qho", "ls", "yd", "st"]
+              + ["k%d" % j for j in range(8)]
+              + ["m%d_%d" % (k, i) for k in range(N) for i in range(4)]
+              + ["r%d_%d" % (k, i) for k in range(2) for i in range(4)]
+              + ["ax%d" % j for j in range(N)] + ["ah%d" % j for j in range(N)]
+              + ["y%d" % j for j in range(N)] + ["c%d" % j for j in range(N)])
+
+
+def roles(T, topo, r):
+    me = T.cores[r]
+    far = [q for q in range(N) if topo.chip(T.cores[q]) != topo.chip(me)]
+    near = [q for q in range(N) if q != r and q not in far]
+    eng, used = {}, set()
+    for j, q in enumerate(far):
+        es = topo.engines(me, T.cores[q])
+        n = len(es) // len(far)
+        eng[q] = es[n * j:n * j + n]
+        used |= set(eng[q])
+    for q in near:
+        eng[q] = [e for e in topo.engines(me, T.cores[q]) if e not in used][::2]
+    return far, near, eng
+
+
+def rank_program(g, core, T, topo):
+    r = T.rank_of(core)
+    if r is None:
+        return
+    S = T.sem
+    V, A = g.vector, g.scalar
+    Copy, Relu = ActivationFunctionType.Copy, ActivationFunctionType.Relu
+    far, near, eng = roles(T, topo, r)
+    order = [r] + near + far
+
+    for k in range(8):
+        q = g.sync if k < 4 else g.scalar
+        q.dma_start(T.trl[16 * k:16 * k + 16, :], T.tri[:]).then_inc(S["tl"], 16)
+    g.sync.dma_start(T.xb[:], T.x[:]).then_inc(S["xl"], 16)
+    g.sync.dma_start(T.wb[:], T.w[:]).then_inc(S["wl"], 16)
+    g.sync.dma_start(T.vb[:], T.vv[:]).then_inc(S["vl"], 16)
+    for k in range(8):
+        g.sync.dma_start(T.plr[16 * k:16 * k + 16, :], T.plt[:]).then_inc(S["pl"], 16)
+
+    V.wait_ge(S["tl"], 128)
+    V.tensor_scalar(T.toff[:], T.trl[:], 0.0, 4.0, AluOpType.max, AluOpType.mult).then_inc(S["tof"], 1)
+    V.wait_ge(S["tof"], 1)
+    V.wait_ge(S["xl"], 16)
+    A.wait_ge(S["tof"], 1)
+    A.wait_ge(S["xl"], 16)
+
+    def gather(on_v, a, n, t, sem):
+        src = T.xb[:, t:2048].indirect(T.toff[:, a * L:(a + n) * L])
+        dst = T.xg[:, a * 4 * C + t:(a + n) * 4 * C:4]
+        if on_v:
+            V.tensor_copy(dst, src).then_inc(S[sem], 1)
+        else:
+            A.activation(dst, src, Copy).then_inc(S[sem], 1)
+
+    def pack_x(a, n, need, sem, done):
+        V.wait_ge(S[sem], need)
+        V.quantize_mx(T.qx[:, a * C:(a + n) * C], T.sx[:, a * C:(a + n) * C],
+                      T.xg[:, a * 4 * C:(a + n) * 4 * C]).then_inc(S[done], 1)
+
+    f0, nf = far[0], len(far)
+    assert far == list(range(f0, f0 + nf)) and len(near) == 1
+    nb = near[0]
+    for t in (0, 1):
+        gather(True, f0, nf, t, "gf")
+    for t in (2, 3):
+        gather(False, f0, nf, t, "gf")
+    pack_x(f0, nf, 4, "gf", "qxf")
+    for t in (0, 1):
+        gather(True, nb, 1, t, "gn")
+    for t in (2, 3):
+        gather(False, nb, 1, t, "gn")
+    pack_x(nb, 1, 4, "gn", "qxn")
+    gather(True, r, 1, 0, "go")
+    for t in (1, 2, 3):
+        gather(False, r, 1, t, "go")
+    pack_x(r, 1, 4, "go", "qxo")
+
+    def tr(q, src, dst, sem):
+        rid, pid = topo.addr(T.cores[q])[:2]
+        return RemoteDMATransfer(dst_ids=[DstId(rid=rid, pnc=pid)], dma_engine_mask=sum(1 << e for e in eng[q]),
+                                 remote_sem=S[sem], src=src, dst=dst)
+
+    def send(codes, plane, lcodes, lplane, sem, ready_far, ready_near):
+        def cut(t, q):
+            return t[:, q * C:(q + 1) * C]
+
+        def ctr(q):
+            return tr(q, cut(codes, q).bitcast(dt.uint8), cut(lcodes, r).bitcast(dt.uint8), sem)
+
+        g.wait_ge(S[ready_far], nf)if ready_far == "qhf" else g.wait_ge(S[ready_far], 1)
+        g.remote_dma_fused([ctr(q) for q in far], local_sem=S["ls"])
+        g.wait_ge(S[ready_near], 1)
+        g.remote_dma_fused([tr(q, cut(plane, q), cut(lplane, r), sem) for q in far + near], local_sem=S["ls"])
+        g.remote_dma_fused([ctr(q) for q in near], local_sem=S["ls"])
+
+    send(T.qx, T.sx, T.rx, T.rsx, "ax%d" % r, "qxf", "qxn")
+
+    V.wait_ge(S["wl"], 16)
+    V.quantize_mx(T.wq[:], T.ws[:], T.wb[:]).then_inc(S["qw"], 1)
+    V.wait_ge(S["vl"], 16)
+    V.quantize_mx(T.vq[:], T.vs[:], T.vb[:]).then_inc(S["qv"], 1)
+
+    arrive = {q: 2 * len(roles(T, topo, q)[2][r]) for q in range(N) if q != r}
+
+    def relu(k, s, i, sem):
+        b = 4 * (k % 2) + i
+        src = T.ps[:, 512 * b:512 * b + C]
+        dst = T.h[:, :, 4 * TR * s + i:4 * TR * (s + 1):4]
+        if i % 2 == 0:
+            V.wait_ge(S["m%d_%d" % (k, i)], 1)
+            V.tensor_scalar(dst, src, 0.0, 0.043, AluOpType.max, AluOpType.mult).then_inc(S[sem], 1)
+        else:
+            A.wait_ge(S["m%d_%d" % (k, i)], 1)
+            A.activation(dst, src, Relu, scale=0.043).then_inc(S[sem], 1)
+
+    def places():
+        V.wait_ge(S["pl"], 128)
+        V.tensor_scalar(T.kf[:], T.plr[:], -0.5 * (TR - 1), 1.0 / TR, AluOpType.add, AluOpType.mult).then_inc(S["k0"], 1)
+        V.wait_ge(S["k0"], 1)
+        V.tensor_copy(T.ki[:], T.kf[:]).then_inc(S["k1"], 1)
+        V.wait_ge(S["k1"], 1)
+        V.tensor_scalar(T.ks[:], T.ki[:], 2, None, AluOpType.arith_shift_right).then_inc(S["k2"], 1)
+        V.tensor_scalar(T.ka[:], T.ki[:], 3, None, AluOpType.bitwise_and).then_inc(S["k2"], 1)
+        V.wait_ge(S["k2"], 2)
+        V.tensor_tensor(T.kd[:], T.ka[:], T.ks[:], AluOpType.subtract).then_inc(S["k3"], 1)
+        V.wait_ge(S["k3"], 1)
+        V.tensor_scalar(T.ke[:], T.kd[:], float(C - TR), None, AluOpType.mult).then_inc(S["k4"], 1)
+        V.wait_ge(S["k4"], 1)
+        V.tensor_tensor(T.kp[:], T.ke[:], T.plr[:], AluOpType.add).then_inc(S["k5"], 1)
+        V.wait_ge(S["k5"], 1)
+        V.tensor_copy(T.poff[:], T.kp[:]).then_inc(S["k6"], 1)
+        V.wait_ge(S["k6"], 1)
+
+    for k, s in enumerate(order):
+        if s == r:
+            g.tensor.wait_ge(S["qw"], 1)
+            g.tensor.wait_ge(S["qxo"], 1)
+            cod, pla = T.qx, T.sx
+        else:
+            g.tensor.wait_ge(S["ax%d" % s], arrive[s])
+            cod, pla = T.rx, T.rsx
+        for i in range(4):
+            b = 4 * (k % 2) + i
+            if k >= 2:
+                g.tensor.wait_ge(S["r%d_%d" % (k - 2, i)], 1)
+            g.tensor.matmul_mx(T.ps[:, 512 * b:512 * b + C], T.wq[:, 128 * i:128 * i + 128], T.ws[:, 128 * i:128 * i + 128],
+                               cod[:, s * C:(s + 1) * C], pla[:, s * C:(s + 1) * C], True, True).then_inc(S["m%d_%d" % (k, i)], 1)
+        for i in range(4):
+            relu(k, s, i, "r%d_%d" % (k, i) if k < 2 else "rr")
+        if k == 0:
+            places()
+
+    V.wait_ge(S["rr"], 8)
+    for q in far + near + [r]:
+        V.quantize_mx(T.qh[:, q * C:(q + 1) * C], T.sh[:, q * C:(q + 1) * C],
+                      T.h[:, q, :]).then_inc(S["qhf" if q in far else "qho" if q == r else "qhn"], 1)
+    send(T.qh, T.sh, T.rh, T.rsh, "ah%d" % r, "qhf", "qhn")
+
+    g.tensor.wait_ge(S["qv"], 1)
+    for k, a in enumerate(order):
+        if a == r:
+            g.tensor.wait_ge(S["qho"], 1)
+            cod, pla = T.qh, T.sh
+        else:
+            g.tensor.wait_ge(S["ah%d" % a], arrive[a])
+            cod, pla = T.rh, T.rsh
+        g.tensor.matmul_mx(T.ps[:, 512 * k:512 * k + C], T.vq[:], T.vs[:],
+                           cod[:, a * C:(a + 1) * C], pla[:, a * C:(a + 1) * C], True, True).then_inc(S["y%d" % k], 1)
+        src, dst = T.ps[:, 512 * k:512 * k + C], T.ysb[:, a * C:(a + 1) * C]
+        if k in (0, 3):
+            V.wait_ge(S["y%d" % k], 1)
+            V.tensor_copy(dst, src).then_inc(S["c%d" % k], 1)
+        else:
+            A.wait_ge(S["y%d" % k], 1)
+            A.activation(dst, src, Copy).then_inc(S["c%d" % k], 1)
+    for e in (V, A):
+        for k in range(N):
+            e.wait_ge(S["c%d" % k], 1)
+    A.wait_ge(S["k6"], 1)
+    V.tensor_copy(T.yo[:, 0:256], T.ysb[:].indirect(T.poff[:, 0:16])).then_inc(S["yd"], 1)
+    A.activation(T.yo[:, 256:512], T.ysb[:].indirect(T.poff[:, 16:32]), Copy).then_inc(S["yd"], 1)
+    g.sync.wait_ge(S["yd"], 2)
+    g.sync.dma_start(T.y[:], T.yo[:]).then_inc(S["st"], 16)
+    g.sync.wait_ge(S["st"], 16)
+    g.wait_ge(S["ls"], 2 * (2 * sum(len(eng[q]) for q in far + near)))

@@ -3,6 +3,7 @@ from concourse.mybir import dt, AluOpType, ActivationFunctionType
 
 N, TR = 4, 40
 C = N * TR
+H = 2 * TR
 W = N * C
 L = C // 16
 F8 = "float8_e4m3fn_x4"
@@ -15,52 +16,54 @@ SCRATCH = {
     "toff": ("sbuf", [128, 40], "uint16"),
     "poff": ("sbuf", [128, 32], "uint16"),
     "kf": ("sbuf", [128, 32], "float32"),
-    "ki": ("sbuf", [128, 32], "int32"),
-    "ks": ("sbuf", [128, 32], "int32"),
-    "ka": ("sbuf", [128, 32], "int32"),
-    "kd": ("sbuf", [128, 32], "int32"),
-    "ke": ("sbuf", [128, 32], "int32"),
-    "kp": ("sbuf", [128, 32], "int32"),
     "xg": ("sbuf", [128, 4 * W], "bfloat16"),
     "qx": ("sbuf", [128, W], F8),
     "sx": ("sbuf", [128, W], "uint8"),
-    "rx": ("sbuf", [128, W], F8),
-    "rsx": ("sbuf", [128, W], "uint8"),
+    "re0": ("sbuf", [128, C], F8),
+    "rse0": ("sbuf", [128, C], "uint8"),
+    "re1": ("sbuf", [128, 2 * C], F8),
+    "rse1": ("sbuf", [128, 2 * C], "uint8"),
     "wq": ("sbuf", [128, 512], F8),
     "ws": ("sbuf", [128, 512], "uint8"),
     "vq": ("sbuf", [128, 128], F8),
     "vs": ("sbuf", [128, 128], "uint8"),
-    "h": ("sbuf", [128, N, 4 * C], "bfloat16"),
-    "qh": ("sbuf", [128, W], F8),
-    "sh": ("sbuf", [128, W], "uint8"),
-    "rh": ("sbuf", [128, W], F8),
-    "rsh": ("sbuf", [128, W], "uint8"),
     "ps": ("psum", [128, 4096], "float32"),
     "ysb": ("sbuf", [128, W], "float32"),
     "yo": ("sbuf", [128, 512], "float32"),
 }
-SEMAPHORES = (["tl", "xl", "wl", "vl", "pl", "tof", "gf", "gn", "go", "qxf", "qxn", "qxo", "qw", "qv",
-               "rr", "qhf", "qhn", "qho", "ls", "yd", "st"]
-              + ["k%d" % j for j in range(8)]
+for _h in range(2):
+    SCRATCH.update({
+        "h%d" % _h: ("sbuf", [128, N, 4 * H], "bfloat16"),
+        "qf%d" % _h: ("sbuf", [128, 2 * H], F8),
+        "sf%d" % _h: ("sbuf", [128, 2 * H], "uint8"),
+        "qo%d" % _h: ("sbuf", [128, 3 * H], F8),
+        "so%d" % _h: ("sbuf", [128, 3 * H], "uint8"),
+        "lf%d" % _h: ("sbuf", [128, 2 * H], F8),
+        "lsf%d" % _h: ("sbuf", [128, 2 * H], "uint8"),
+    })
+for _j in range(13):
+    SCRATCH["t%d" % _j] = ("sbuf", [128, 32], "int32")
+SEMAPHORES = (["tl", "xl", "wl", "vl", "pl", "tof", "qw", "qv", "rf", "rn", "ls", "yd0", "yd1", "st"]
+              + ["g%d" % j for j in range(N)] + ["qx%d" % j for j in range(N)]
+              + ["qhf%d" % j for j in range(2)] + ["qho%d" % j for j in range(2)]
+              + ["k%d" % j for j in range(15)]
               + ["m%d_%d" % (k, i) for k in range(N) for i in range(4)]
               + ["r%d_%d" % (k, i) for k in range(2) for i in range(4)]
-              + ["ax%d" % j for j in range(N)] + ["ah%d" % j for j in range(N)]
+              + ["ax%d" % j for j in range(N)] + ["ah%d_%d" % (h, j) for h in range(2) for j in range(N)]
               + ["y%d" % j for j in range(N)] + ["c%d" % j for j in range(N)])
 
 
 def roles(T, topo, r):
     me = T.cores[r]
     far = [q for q in range(N) if topo.chip(T.cores[q]) != topo.chip(me)]
-    near = [q for q in range(N) if q != r and q not in far]
-    eng, used = {}, set()
-    for j, q in enumerate(far):
-        es = topo.engines(me, T.cores[q])
-        n = len(es) // len(far)
-        eng[q] = es[n * j:n * j + n]
-        used |= set(eng[q])
-    for q in near:
-        eng[q] = [e for e in topo.engines(me, T.cores[q]) if e not in used][::2]
-    return far, near, eng
+    far.sort(key=lambda q: (q % 2 != r % 2, q))
+    near = [q for q in range(N) if q != r and q not in far][0]
+    out = topo.engines(me, T.cores[far[0]])
+    half = len(out) // 2
+    inside = [e for e in topo.engines(me, T.cores[near]) if e not in out]
+    hop1 = {far[0]: out, far[1]: out, near: inside}
+    hop2 = {far[0]: out[:half], far[1]: out[half:], near: inside}
+    return far, near, hop1, hop2
 
 
 def rank_program(g, core, T, topo):
@@ -68,13 +71,16 @@ def rank_program(g, core, T, topo):
     if r is None:
         return
     S = T.sem
-    V, A = g.vector, g.scalar
-    Copy, Relu = ActivationFunctionType.Copy, ActivationFunctionType.Relu
-    far, near, eng = roles(T, topo, r)
-    order = [r] + near + far
+    V, A, P = g.vector, g.scalar, g.tensor
+    Copy, Relu, M = ActivationFunctionType.Copy, ActivationFunctionType.Relu, AluOpType
+    far, near, hop1, hop2 = roles(T, topo, r)
+    early, late = far
+    f0, o0 = 2 * (far[0] // 2), 2 * (r // 2)
+    assert sorted(far) == [f0, f0 + 1] and sorted([r, near]) == [o0, o0 + 1]
+    odd = r % 2
 
     for k in range(8):
-        q = g.sync if k < 4 else g.scalar
+        q = g.sync if k < 4 else A
         q.dma_start(T.trl[16 * k:16 * k + 16, :], T.tri[:]).then_inc(S["tl"], 16)
     g.sync.dma_start(T.xb[:], T.x[:]).then_inc(S["xl"], 16)
     g.sync.dma_start(T.wb[:], T.w[:]).then_inc(S["wl"], 16)
@@ -83,148 +89,190 @@ def rank_program(g, core, T, topo):
         g.sync.dma_start(T.plr[16 * k:16 * k + 16, :], T.plt[:]).then_inc(S["pl"], 16)
 
     V.wait_ge(S["tl"], 128)
-    V.tensor_scalar(T.toff[:], T.trl[:], 0.0, 4.0, AluOpType.max, AluOpType.mult).then_inc(S["tof"], 1)
-    V.wait_ge(S["tof"], 1)
-    V.wait_ge(S["xl"], 16)
-    A.wait_ge(S["tof"], 1)
-    A.wait_ge(S["xl"], 16)
+    V.tensor_scalar(T.toff[:], T.trl[:], 0.0, 4.0, M.max, M.mult).then_inc(S["tof"], 1)
+    for e in (V, A):
+        e.wait_ge(S["tof"], 1)
+        e.wait_ge(S["xl"], 16)
 
-    def gather(on_v, a, n, t, sem):
-        src = T.xb[:, t:2048].indirect(T.toff[:, a * L:(a + n) * L])
-        dst = T.xg[:, a * 4 * C + t:(a + n) * 4 * C:4]
-        if on_v:
-            V.tensor_copy(dst, src).then_inc(S[sem], 1)
-        else:
-            A.activation(dst, src, Copy).then_inc(S[sem], 1)
+    def gather(a, nv):
+        for t in range(4):
+            src = T.xb[:, t:2048].indirect(T.toff[:, a * L:(a + 1) * L])
+            dst = T.xg[:, a * 4 * C + t:(a + 1) * 4 * C:4]
+            if t < nv:
+                V.tensor_copy(dst, src).then_inc(S["g%d" % a], 1)
+            else:
+                A.activation(dst, src, Copy).then_inc(S["g%d" % a], 1)
 
-    def pack_x(a, n, need, sem, done):
-        V.wait_ge(S[sem], need)
-        V.quantize_mx(T.qx[:, a * C:(a + n) * C], T.sx[:, a * C:(a + n) * C],
-                      T.xg[:, a * 4 * C:(a + n) * 4 * C]).then_inc(S[done], 1)
+    def pack(a):
+        V.wait_ge(S["g%d" % a], 4)
+        V.quantize_mx(T.qx[:, a * C:(a + 1) * C], T.sx[:, a * C:(a + 1) * C],
+                      T.xg[:, a * 4 * C:(a + 1) * 4 * C]).then_inc(S["qx%d" % a], 1)
 
-    f0, nf = far[0], len(far)
-    assert far == list(range(f0, f0 + nf)) and len(near) == 1
-    nb = near[0]
-    for t in (0, 1):
-        gather(True, f0, nf, t, "gf")
-    for t in (2, 3):
-        gather(False, f0, nf, t, "gf")
-    pack_x(f0, nf, 4, "gf", "qxf")
-    for t in (0, 1):
-        gather(True, nb, 1, t, "gn")
-    for t in (2, 3):
-        gather(False, nb, 1, t, "gn")
-    pack_x(nb, 1, 4, "gn", "qxn")
-    gather(True, r, 1, 0, "go")
-    for t in (1, 2, 3):
-        gather(False, r, 1, t, "go")
-    pack_x(r, 1, 4, "go", "qxo")
-
-    def tr(q, src, dst, sem):
-        rid, pid = topo.addr(T.cores[q])[:2]
-        return RemoteDMATransfer(dst_ids=[DstId(rid=rid, pnc=pid)], dma_engine_mask=sum(1 << e for e in eng[q]),
-                                 remote_sem=S[sem], src=src, dst=dst)
-
-    def send(codes, plane, lcodes, lplane, sem, ready_far, ready_near):
-        def cut(t, q):
-            return t[:, q * C:(q + 1) * C]
-
-        def ctr(q):
-            return tr(q, cut(codes, q).bitcast(dt.uint8), cut(lcodes, r).bitcast(dt.uint8), sem)
-
-        g.wait_ge(S[ready_far], nf)if ready_far == "qhf" else g.wait_ge(S[ready_far], 1)
-        g.remote_dma_fused([ctr(q) for q in far], local_sem=S["ls"])
-        g.wait_ge(S[ready_near], 1)
-        g.remote_dma_fused([tr(q, cut(plane, q), cut(lplane, r), sem) for q in far + near], local_sem=S["ls"])
-        g.remote_dma_fused([ctr(q) for q in near], local_sem=S["ls"])
-
-    send(T.qx, T.sx, T.rx, T.rsx, "ax%d" % r, "qxf", "qxn")
-
+    for a, nv in ((early, 2), (near, 2), (late, 1)):
+        gather(a, nv)
+        pack(a)
+    gather(r, 1)
     V.wait_ge(S["wl"], 16)
     V.quantize_mx(T.wq[:], T.ws[:], T.wb[:]).then_inc(S["qw"], 1)
+    pack(r)
     V.wait_ge(S["vl"], 16)
     V.quantize_mx(T.vq[:], T.vs[:], T.vb[:]).then_inc(S["qv"], 1)
 
-    arrive = {q: 2 * len(roles(T, topo, q)[2][r]) for q in range(N) if q != r}
+    def fire(qs, eng, sem, src, dst):
+        trs = []
+        for q in qs:
+            rid, pid = topo.addr(T.cores[q])[:2]
+            trs.append(RemoteDMATransfer(dst_ids=[DstId(rid=rid, pnc=pid)], dma_engine_mask=sum(1 << e for e in eng[q]),
+                                         remote_sem=S[sem], src=src(q), dst=dst(q)))
+        g.remote_dma_fused(trs, local_sem=S["ls"])
 
-    def relu(k, s, i, sem):
-        b = 4 * (k % 2) + i
-        src = T.ps[:, 512 * b:512 * b + C]
-        dst = T.h[:, :, 4 * TR * s + i:4 * TR * (s + 1):4]
-        if i % 2 == 0:
-            V.wait_ge(S["m%d_%d" % (k, i)], 1)
-            V.tensor_scalar(dst, src, 0.0, 0.043, AluOpType.max, AluOpType.mult).then_inc(S[sem], 1)
-        else:
-            A.wait_ge(S["m%d_%d" % (k, i)], 1)
-            A.activation(dst, src, Relu, scale=0.043).then_inc(S[sem], 1)
+    runs = {early: [(0, 0, C)], late: [(0, H, C)], near: [(0, 0, H), (H, 3 * H, H)]}
+    for a in (early, near, late):
+        h = 0 if a == early else 1
+        lq, lp, b = T["re%d" % h], T["rse%d" % h], a * C
+        g.wait_ge(S["qx%d" % a], 1)
+        for u, v, n in runs[a]:
+            fire([a], hop1, "ax%d" % r, lambda q: T.qx[:, b + u:b + u + n].bitcast(dt.uint8),
+                 lambda q: lq[:, v:v + n].bitcast(dt.uint8))
+        for u, v, n in runs[a]:
+            fire([a], hop1, "ax%d" % r, lambda q: T.sx[:, b + u:b + u + n], lambda q: lp[:, v:v + n])
 
-    def places():
-        V.wait_ge(S["pl"], 128)
-        V.tensor_scalar(T.kf[:], T.plr[:], -0.5 * (TR - 1), 1.0 / TR, AluOpType.add, AluOpType.mult).then_inc(S["k0"], 1)
-        V.wait_ge(S["k0"], 1)
-        V.tensor_copy(T.ki[:], T.kf[:]).then_inc(S["k1"], 1)
-        V.wait_ge(S["k1"], 1)
-        V.tensor_scalar(T.ks[:], T.ki[:], 2, None, AluOpType.arith_shift_right).then_inc(S["k2"], 1)
-        V.tensor_scalar(T.ka[:], T.ki[:], 3, None, AluOpType.bitwise_and).then_inc(S["k2"], 1)
-        V.wait_ge(S["k2"], 2)
-        V.tensor_tensor(T.kd[:], T.ka[:], T.ks[:], AluOpType.subtract).then_inc(S["k3"], 1)
-        V.wait_ge(S["k3"], 1)
-        V.tensor_scalar(T.ke[:], T.kd[:], float(C - TR), None, AluOpType.mult).then_inc(S["k4"], 1)
-        V.wait_ge(S["k4"], 1)
-        V.tensor_tensor(T.kp[:], T.ke[:], T.plr[:], AluOpType.add).then_inc(S["k5"], 1)
-        V.wait_ge(S["k5"], 1)
-        V.tensor_copy(T.poff[:], T.kp[:]).then_inc(S["k6"], 1)
-        V.wait_ge(S["k6"], 1)
+    def landed(s):
+        n = 4 if s == near else 2
+        P.wait_ge(S["ax%d" % s], n * len(roles(T, topo, s)[2][r]))
 
-    for k, s in enumerate(order):
-        if s == r:
-            g.tensor.wait_ge(S["qw"], 1)
-            g.tensor.wait_ge(S["qxo"], 1)
-            cod, pla = T.qx, T.sx
-        else:
-            g.tensor.wait_ge(S["ax%d" % s], arrive[s])
-            cod, pla = T.rx, T.rsx
+    ts, tt = V.tensor_scalar, V.tensor_tensor
+    todo = [
+        (ts, (T.kf[:], T.plr[:], -0.5 * (TR - 1), 1.0 / TR, M.add, M.mult), ()),
+        (V.tensor_copy, (T.t0[:], T.kf[:]), (0,)),
+        (ts, (T.t1[:], T.t0[:], 3, None, M.arith_shift_right), (1,)),
+        (ts, (T.t2[:], T.t0[:], 2, 1, M.arith_shift_right, M.bitwise_and), (1,)),
+        (ts, (T.t3[:], T.t0[:], 1, None, M.bitwise_and), (1,)),
+        (ts, (T.t5[:], T.t0[:], 40.0, 80.0, M.mult, M.add), (1,)),
+        (tt, (T.t4[:], T.t2[:], T.t3[:], M.mult), (3, 4)),
+        (ts, (T.t6[:], T.t1[:], -600.0, None, M.mult), (2,)),
+        (ts, (T.t8[:], T.t3[:], 160.0, None, M.mult), (4,)),
+        (tt, (T.t9[:], T.plr[:], T.t5[:], M.add), (5,)),
+        (ts, (T.t7[:], T.t4[:], -640.0, None, M.mult), (6,)),
+        (tt, (T.t10[:], T.t6[:], T.t8[:], M.add), (7, 8)),
+        (tt, (T.t11[:], T.t10[:], T.t7[:], M.add), (10, 11)),
+        (tt, (T.t12[:], T.t9[:], T.t11[:], M.add), (9, 12)),
+        (V.tensor_copy, (T.poff[:], T.t12[:]), (13,)),
+    ]
+    done = [0]
+
+    def places(n):
+        for _ in range(n):
+            call, args, need = todo[done[0]]
+            if done[0] == 0:
+                V.wait_ge(S["pl"], 128)
+            for k in need:
+                V.wait_ge(S["k%d" % k], 1)
+            call(*args).then_inc(S["k%d" % done[0]], 1)
+            done[0] += 1
+
+    def product(k, cod, pla, c0):
         for i in range(4):
             b = 4 * (k % 2) + i
             if k >= 2:
-                g.tensor.wait_ge(S["r%d_%d" % (k - 2, i)], 1)
-            g.tensor.matmul_mx(T.ps[:, 512 * b:512 * b + C], T.wq[:, 128 * i:128 * i + 128], T.ws[:, 128 * i:128 * i + 128],
-                               cod[:, s * C:(s + 1) * C], pla[:, s * C:(s + 1) * C], True, True).then_inc(S["m%d_%d" % (k, i)], 1)
+                P.wait_ge(S["r%d_%d" % (k - 2, i)], 1)
+            P.matmul_mx(T.ps[:, 512 * b:512 * b + C], T.wq[:, 128 * i:128 * i + 128], T.ws[:, 128 * i:128 * i + 128],
+                        cod[:, c0:c0 + C], pla[:, c0:c0 + C], True, True).then_inc(S["m%d_%d" % (k, i)], 1)
+
+    def relu(k, i, pieces, hh, sem):
+        b = 512 * (4 * (k % 2) + i)
+        e = V if i % 2 else A
+        e.wait_ge(S["m%d_%d" % (k, i)], 1)
+        for c0, n, s, b0, b1 in pieces:
+            src = T.ps[:, b + c0:b + c0 + n]
+            dst = hh[:, b0:b1, 4 * TR * (s // 2) + i:4 * TR * (s // 2 + 1):4]
+            if e is A:
+                c = A.activation(dst, src, Relu, scale=0.043)
+            else:
+                c = V.tensor_scalar(dst, src, 0.0, 0.043, M.max, M.mult)
+            c.then_inc(S[sem], 1)
+
+    ow = 0 if odd else H
+    at = 0 if odd else 2 * H
+    view = H if odd else 0
+
+    def onward_far(h):
+        hh, qf, sf, lf, lsf = (T["%s%d" % (n, h)] for n in ("h", "qf", "sf", "lf", "lsf"))
+        sem, fl = "ah%d_%d" % (h, r), H * (1 - odd)
+        V.quantize_mx(qf[:], sf[:], hh[:, f0:f0 + 2, :]).then_inc(S["qhf%d" % h], 1)
+        g.wait_ge(S["qhf%d" % h], 1)
+        fire(far, hop2, sem, lambda q: qf[:, H * (q % 2):H * (q % 2) + H].bitcast(dt.uint8),
+             lambda q: lf[:, fl:fl + H].bitcast(dt.uint8))
+        fire(far, hop2, sem, lambda q: sf[:, H * (q % 2):H * (q % 2) + H], lambda q: lsf[:, fl:fl + H])
+
+    def onward_near(h):
+        hh, qo, so = (T["%s%d" % (n, h)] for n in ("h", "qo", "so"))
+        sem = "ah%d_%d" % (h, r)
+        V.quantize_mx(qo[:, ow:ow + 2 * H], so[:, ow:ow + 2 * H], hh[:, o0:o0 + 2, :]).then_inc(S["qho%d" % h], 1)
+        g.wait_ge(S["qho%d" % h], 1)
+        fire([near], hop2, sem, lambda q: qo[:, at:at + H].bitcast(dt.uint8), lambda q: qo[:, at:at + H].bitcast(dt.uint8))
+        fire([near], hop2, sem, lambda q: so[:, at:at + H], lambda q: so[:, at:at + H])
+
+    P.wait_ge(S["qw"], 1)
+    P.wait_ge(S["qx%d" % r], 1)
+    product(0, T.qx, T.sx, r * C)
+    landed(early)
+    product(1, T.re0, T.rse0, 0)
+    landed(near)
+    landed(late)
+    product(2, T.re1, T.rse1, f0 // 2 * C)
+    product(3, T.re1, T.rse1, o0 // 2 * C)
+
+    for k, s in ((0, r), (1, early)):
         for i in range(4):
-            relu(k, s, i, "r%d_%d" % (k, i) if k < 2 else "rr")
-        if k == 0:
-            places()
+            relu(k, i, [(0, C, s, 0, N)], T.h0, "r%d_%d" % (k, i))
+            if i % 2:
+                places(2)
+    for k in range(2):
+        for i in range(4):
+            V.wait_ge(S["r%d_%d" % (k, i)], 1)
+    onward_far(0)
+    onward_near(0)
 
-    V.wait_ge(S["rr"], 8)
-    for q in far + near + [r]:
-        V.quantize_mx(T.qh[:, q * C:(q + 1) * C], T.sh[:, q * C:(q + 1) * C],
-                      T.h[:, q, :]).then_inc(S["qhf" if q in far else "qho" if q == r else "qhn"], 1)
-    send(T.qh, T.sh, T.rh, T.rsh, "ah%d" % r, "qhf", "qhn")
+    def half1(k, p, sem):
+        for i in range(4):
+            two = (near, late) if p == 0 else (late, near)
+            relu(k, i, [(H * j, H, s, p, p + 2) for j, s in enumerate(two)], T.h1, sem)
+        V.wait_ge(S[sem], 8)
 
-    g.tensor.wait_ge(S["qv"], 1)
-    for k, a in enumerate(order):
-        if a == r:
-            g.tensor.wait_ge(S["qho"], 1)
-            cod, pla = T.qh, T.sh
+    half1(2, f0, "rf")
+    onward_far(1)
+    half1(3, o0, "rn")
+    onward_near(1)
+    places(len(todo) - done[0])
+
+    P.wait_ge(S["qv"], 1)
+    for h in range(2):
+        P.wait_ge(S["qho%d" % h], 1)
+    for k in range(4):
+        h, out = k // 2, k % 2
+        if out:
+            cod, pla, c0, base = T["lf%d" % h], T["lsf%d" % h], 0, f0
         else:
-            g.tensor.wait_ge(S["ah%d" % a], arrive[a])
-            cod, pla = T.rh, T.rsh
-        g.tensor.matmul_mx(T.ps[:, 512 * k:512 * k + C], T.vq[:], T.vs[:],
-                           cod[:, a * C:(a + 1) * C], pla[:, a * C:(a + 1) * C], True, True).then_inc(S["y%d" % k], 1)
-        src, dst = T.ps[:, 512 * k:512 * k + C], T.ysb[:, a * C:(a + 1) * C]
-        if k in (0, 3):
-            V.wait_ge(S["y%d" % k], 1)
-            V.tensor_copy(dst, src).then_inc(S["c%d" % k], 1)
-        else:
-            A.wait_ge(S["y%d" % k], 1)
-            A.activation(dst, src, Copy).then_inc(S["c%d" % k], 1)
+            cod, pla, c0, base = T["qo%d" % h], T["so%d" % h], view, o0
+        for a in (far if out else [near]):
+            P.wait_ge(S["ah%d_%d" % (h, a)], 2 * len(roles(T, topo, a)[3][r]))
+        P.matmul_mx(T.ps[:, 512 * k:512 * k + C], T.vq[:], T.vs[:],
+                    cod[:, c0:c0 + C], pla[:, c0:c0 + C], True, True).then_inc(S["y%d" % k], 1)
+        p = 2 * C * h + C * (base // 2)
+        src, dst = T.ps[:, 512 * k:512 * k + C], T.ysb[:, p:p + C]
+        e = V if k == 3 else A
+        e.wait_ge(S["y%d" % k], 1)
+        (V.tensor_copy(dst, src) if e is V else A.activation(dst, src, Copy)).then_inc(S["c%d" % k], 1)
     for e in (V, A):
+        e.wait_ge(S["k14"], 1)
         for k in range(N):
             e.wait_ge(S["c%d" % k], 1)
-    A.wait_ge(S["k6"], 1)
-    V.tensor_copy(T.yo[:, 0:256], T.ysb[:].indirect(T.poff[:, 0:16])).then_inc(S["yd"], 1)
-    A.activation(T.yo[:, 256:512], T.ysb[:].indirect(T.poff[:, 16:32]), Copy).then_inc(S["yd"], 1)
-    g.sync.wait_ge(S["yd"], 2)
-    g.sync.dma_start(T.y[:], T.yo[:]).then_inc(S["st"], 16)
-    g.sync.wait_ge(S["st"], 16)
-    g.wait_ge(S["ls"], 2 * (2 * sum(len(eng[q]) for q in far + near)))
+    for j in range(2):
+        a = 256 * j
+        V.tensor_copy(T.yo[:, a:a + 128], T.ysb[:].indirect(T.poff[:, a // 16:a // 16 + 8])).then_inc(S["yd%d" % j], 1)
+        A.activation(T.yo[:, a + 128:a + 256], T.ysb[:].indirect(T.poff[:, a // 16 + 8:a // 16 + 16]), Copy).then_inc(S["yd%d" % j], 1)
+        g.sync.wait_ge(S["yd%d" % j], 2)
+        g.sync.dma_start(T.y[:, a:a + 256], T.yo[:, a:a + 256]).then_inc(S["st"], 16)
+    g.sync.wait_ge(S["st"], 32)
+    g.wait_ge(S["ls"], 2 * sum(len(hop1[q]) * len(runs[q]) for q in hop1) + 4 * sum(len(e) for e in hop2.values()))

from concourse.bass import DstId, RemoteDMATransfer
from concourse.mybir import dt, AluOpType, ActivationFunctionType

N, TR = 4, 40
C = N * TR
H = 2 * TR
W = N * C
L = C // 16
F8 = "float8_e4m3fn_x4"
SCRATCH = {
    "xb": ("sbuf", [128, 2048], "bfloat16"),
    "wb": ("sbuf", [128, 2048], "bfloat16"),
    "vb": ("sbuf", [128, 512], "bfloat16"),
    "trl": ("sbuf", [128, 40], "int32"),
    "plr": ("sbuf", [128, 32], "int32"),
    "toff": ("sbuf", [128, 40], "uint16"),
    "poff": ("sbuf", [128, 32], "uint16"),
    "kf": ("sbuf", [128, 32], "float32"),
    "xg": ("sbuf", [128, 4 * W], "bfloat16"),
    "qx": ("sbuf", [128, W], F8),
    "sx": ("sbuf", [128, W], "uint8"),
    "re0": ("sbuf", [128, C], F8),
    "rse0": ("sbuf", [128, C], "uint8"),
    "re1": ("sbuf", [128, 2 * C], F8),
    "rse1": ("sbuf", [128, 2 * C], "uint8"),
    "wq": ("sbuf", [128, 512], F8),
    "ws": ("sbuf", [128, 512], "uint8"),
    "vq": ("sbuf", [128, 128], F8),
    "vs": ("sbuf", [128, 128], "uint8"),
    "ps": ("psum", [128, 4096], "float32"),
    "ysb": ("sbuf", [128, W], "float32"),
    "yo": ("sbuf", [128, 512], "float32"),
}
for _h in range(2):
    SCRATCH.update({
        "h%d" % _h: ("sbuf", [128, N, 4 * H], "bfloat16"),
        "qf%d" % _h: ("sbuf", [128, 2 * H], F8),
        "sf%d" % _h: ("sbuf", [128, 2 * H], "uint8"),
        "qo%d" % _h: ("sbuf", [128, 3 * H], F8),
        "so%d" % _h: ("sbuf", [128, 3 * H], "uint8"),
        "lf%d" % _h: ("sbuf", [128, 2 * H], F8),
        "lsf%d" % _h: ("sbuf", [128, 2 * H], "uint8"),
    })
for _j in range(13):
    SCRATCH["t%d" % _j] = ("sbuf", [128, 32], "int32")
SEMAPHORES = (["tl", "xl", "wl", "vl", "pl", "tof", "qw", "qv", "rf", "rn", "ls", "yd0", "yd1", "st"]
              + ["g%d" % j for j in range(N)] + ["qx%d" % j for j in range(N)]
              + ["qhf%d" % j for j in range(2)] + ["qho%d" % j for j in range(2)]
              + ["k%d" % j for j in range(15)]
              + ["m%d_%d" % (k, i) for k in range(N) for i in range(4)]
              + ["r%d_%d" % (k, i) for k in range(2) for i in range(4)]
              + ["ax%d" % j for j in range(N)] + ["ah%d_%d" % (h, j) for h in range(2) for j in range(N)]
              + ["y%d" % j for j in range(N)] + ["c%d" % j for j in range(N)])


def roles(T, topo, r):
    me = T.cores[r]
    far = [q for q in range(N) if topo.chip(T.cores[q]) != topo.chip(me)]
    far.sort(key=lambda q: (q % 2 != r % 2, q))
    near = [q for q in range(N) if q != r and q not in far][0]
    out = topo.engines(me, T.cores[far[0]])
    half = len(out) // 2
    inside = [e for e in topo.engines(me, T.cores[near]) if e not in out]
    hop1 = {far[0]: out, far[1]: out, near: inside}
    hop2 = {far[0]: out[:half], far[1]: out[half:], near: inside}
    return far, near, hop1, hop2


def rank_program(g, core, T, topo):
    r = T.rank_of(core)
    if r is None:
        return
    S = T.sem
    V, A, P = g.vector, g.scalar, g.tensor
    Copy, Relu, M = ActivationFunctionType.Copy, ActivationFunctionType.Relu, AluOpType
    far, near, hop1, hop2 = roles(T, topo, r)
    early, late = far
    f0, o0 = 2 * (far[0] // 2), 2 * (r // 2)
    assert sorted(far) == [f0, f0 + 1] and sorted([r, near]) == [o0, o0 + 1]
    odd = r % 2

    for k in range(8):
        q = g.sync if k < 4 else A
        q.dma_start(T.trl[16 * k:16 * k + 16, :], T.tri[:]).then_inc(S["tl"], 16)
    g.sync.dma_start(T.xb[:], T.x[:]).then_inc(S["xl"], 16)
    g.sync.dma_start(T.wb[:], T.w[:]).then_inc(S["wl"], 16)
    g.sync.dma_start(T.vb[:], T.vv[:]).then_inc(S["vl"], 16)
    for k in range(8):
        g.sync.dma_start(T.plr[16 * k:16 * k + 16, :], T.plt[:]).then_inc(S["pl"], 16)

    V.wait_ge(S["tl"], 128)
    V.tensor_scalar(T.toff[:], T.trl[:], 0.0, 4.0, M.max, M.mult).then_inc(S["tof"], 1)
    for e in (V, A):
        e.wait_ge(S["tof"], 1)
        e.wait_ge(S["xl"], 16)

    def gather(a, nv):
        for t in range(4):
            src = T.xb[:, t:2048].indirect(T.toff[:, a * L:(a + 1) * L])
            dst = T.xg[:, a * 4 * C + t:(a + 1) * 4 * C:4]
            if t < nv:
                V.tensor_copy(dst, src).then_inc(S["g%d" % a], 1)
            else:
                A.activation(dst, src, Copy).then_inc(S["g%d" % a], 1)

    def pack(a):
        V.wait_ge(S["g%d" % a], 4)
        V.quantize_mx(T.qx[:, a * C:(a + 1) * C], T.sx[:, a * C:(a + 1) * C],
                      T.xg[:, a * 4 * C:(a + 1) * 4 * C]).then_inc(S["qx%d" % a], 1)

    for a, nv in ((early, 2), (near, 2), (late, 1)):
        gather(a, nv)
        pack(a)
    gather(r, 1)
    V.wait_ge(S["wl"], 16)
    V.quantize_mx(T.wq[:], T.ws[:], T.wb[:]).then_inc(S["qw"], 1)
    pack(r)
    V.wait_ge(S["vl"], 16)
    V.quantize_mx(T.vq[:], T.vs[:], T.vb[:]).then_inc(S["qv"], 1)

    def fire(qs, eng, sem, src, dst):
        trs = []
        for q in qs:
            rid, pid = topo.addr(T.cores[q])[:2]
            trs.append(RemoteDMATransfer(dst_ids=[DstId(rid=rid, pnc=pid)], dma_engine_mask=sum(1 << e for e in eng[q]),
                                         remote_sem=S[sem], src=src(q), dst=dst(q)))
        g.remote_dma_fused(trs, local_sem=S["ls"])

    runs = {early: [(0, 0, C)], late: [(0, H, C)], near: [(0, 0, H), (H, 3 * H, H)]}
    for a in (early, near, late):
        h = 0 if a == early else 1
        lq, lp, b = T["re%d" % h], T["rse%d" % h], a * C
        g.wait_ge(S["qx%d" % a], 1)
        for u, v, n in runs[a]:
            fire([a], hop1, "ax%d" % r, lambda q: T.qx[:, b + u:b + u + n].bitcast(dt.uint8),
                 lambda q: lq[:, v:v + n].bitcast(dt.uint8))
        for u, v, n in runs[a]:
            fire([a], hop1, "ax%d" % r, lambda q: T.sx[:, b + u:b + u + n], lambda q: lp[:, v:v + n])

    def landed(s):
        n = 4 if s == near else 2
        P.wait_ge(S["ax%d" % s], n * len(roles(T, topo, s)[2][r]))

    ts, tt = V.tensor_scalar, V.tensor_tensor
    todo = [
        (ts, (T.kf[:], T.plr[:], -0.5 * (TR - 1), 1.0 / TR, M.add, M.mult), ()),
        (V.tensor_copy, (T.t0[:], T.kf[:]), (0,)),
        (ts, (T.t1[:], T.t0[:], 3, None, M.arith_shift_right), (1,)),
        (ts, (T.t2[:], T.t0[:], 2, 1, M.arith_shift_right, M.bitwise_and), (1,)),
        (ts, (T.t3[:], T.t0[:], 1, None, M.bitwise_and), (1,)),
        (ts, (T.t5[:], T.t0[:], 40.0, 80.0, M.mult, M.add), (1,)),
        (tt, (T.t4[:], T.t2[:], T.t3[:], M.mult), (3, 4)),
        (ts, (T.t6[:], T.t1[:], -600.0, None, M.mult), (2,)),
        (ts, (T.t8[:], T.t3[:], 160.0, None, M.mult), (4,)),
        (tt, (T.t9[:], T.plr[:], T.t5[:], M.add), (5,)),
        (ts, (T.t7[:], T.t4[:], -640.0, None, M.mult), (6,)),
        (tt, (T.t10[:], T.t6[:], T.t8[:], M.add), (7, 8)),
        (tt, (T.t11[:], T.t10[:], T.t7[:], M.add), (10, 11)),
        (tt, (T.t12[:], T.t9[:], T.t11[:], M.add), (9, 12)),
        (V.tensor_copy, (T.poff[:], T.t12[:]), (13,)),
    ]
    done = [0]

    def places(n):
        for _ in range(n):
            call, args, need = todo[done[0]]
            if done[0] == 0:
                V.wait_ge(S["pl"], 128)
            for k in need:
                V.wait_ge(S["k%d" % k], 1)
            call(*args).then_inc(S["k%d" % done[0]], 1)
            done[0] += 1

    def product(k, cod, pla, c0):
        for i in range(4):
            b = 4 * (k % 2) + i
            if k >= 2:
                P.wait_ge(S["r%d_%d" % (k - 2, i)], 1)
            P.matmul_mx(T.ps[:, 512 * b:512 * b + C], T.wq[:, 128 * i:128 * i + 128], T.ws[:, 128 * i:128 * i + 128],
                        cod[:, c0:c0 + C], pla[:, c0:c0 + C], True, True).then_inc(S["m%d_%d" % (k, i)], 1)

    def relu(k, i, pieces, hh, sem):
        b = 512 * (4 * (k % 2) + i)
        e = V if i % 2 else A
        e.wait_ge(S["m%d_%d" % (k, i)], 1)
        for c0, n, s, b0, b1 in pieces:
            src = T.ps[:, b + c0:b + c0 + n]
            dst = hh[:, b0:b1, 4 * TR * (s // 2) + i:4 * TR * (s // 2 + 1):4]
            if e is A:
                c = A.activation(dst, src, Relu, scale=0.043)
            else:
                c = V.tensor_scalar(dst, src, 0.0, 0.043, M.max, M.mult)
            c.then_inc(S[sem], 1)

    ow = 0 if odd else H
    at = 0 if odd else 2 * H
    view = H if odd else 0

    def onward_far(h):
        hh, qf, sf, lf, lsf = (T["%s%d" % (n, h)] for n in ("h", "qf", "sf", "lf", "lsf"))
        sem, fl = "ah%d_%d" % (h, r), H * (1 - odd)
        V.quantize_mx(qf[:], sf[:], hh[:, f0:f0 + 2, :]).then_inc(S["qhf%d" % h], 1)
        g.wait_ge(S["qhf%d" % h], 1)
        fire(far, hop2, sem, lambda q: qf[:, H * (q % 2):H * (q % 2) + H].bitcast(dt.uint8),
             lambda q: lf[:, fl:fl + H].bitcast(dt.uint8))
        fire(far, hop2, sem, lambda q: sf[:, H * (q % 2):H * (q % 2) + H], lambda q: lsf[:, fl:fl + H])

    def onward_near(h):
        hh, qo, so = (T["%s%d" % (n, h)] for n in ("h", "qo", "so"))
        sem = "ah%d_%d" % (h, r)
        V.quantize_mx(qo[:, ow:ow + 2 * H], so[:, ow:ow + 2 * H], hh[:, o0:o0 + 2, :]).then_inc(S["qho%d" % h], 1)
        g.wait_ge(S["qho%d" % h], 1)
        fire([near], hop2, sem, lambda q: qo[:, at:at + H].bitcast(dt.uint8), lambda q: qo[:, at:at + H].bitcast(dt.uint8))
        fire([near], hop2, sem, lambda q: so[:, at:at + H], lambda q: so[:, at:at + H])

    P.wait_ge(S["qw"], 1)
    P.wait_ge(S["qx%d" % r], 1)
    product(0, T.qx, T.sx, r * C)
    landed(early)
    product(1, T.re0, T.rse0, 0)
    landed(near)
    landed(late)
    product(2, T.re1, T.rse1, f0 // 2 * C)
    product(3, T.re1, T.rse1, o0 // 2 * C)

    for k, s in ((0, r), (1, early)):
        for i in range(4):
            relu(k, i, [(0, C, s, 0, N)], T.h0, "r%d_%d" % (k, i))
            if i % 2:
                places(2)
    for k in range(2):
        for i in range(4):
            V.wait_ge(S["r%d_%d" % (k, i)], 1)
    onward_far(0)
    onward_near(0)

    def half1(k, p, sem):
        for i in range(4):
            two = (near, late) if p == 0 else (late, near)
            relu(k, i, [(H * j, H, s, p, p + 2) for j, s in enumerate(two)], T.h1, sem)
        V.wait_ge(S[sem], 8)

    half1(2, f0, "rf")
    onward_far(1)
    half1(3, o0, "rn")
    onward_near(1)
    places(len(todo) - done[0])

    P.wait_ge(S["qv"], 1)
    for h in range(2):
        P.wait_ge(S["qho%d" % h], 1)
    for k in range(4):
        h, out = k // 2, k % 2
        if out:
            cod, pla, c0, base = T["lf%d" % h], T["lsf%d" % h], 0, f0
        else:
            cod, pla, c0, base = T["qo%d" % h], T["so%d" % h], view, o0
        for a in (far if out else [near]):
            P.wait_ge(S["ah%d_%d" % (h, a)], 2 * len(roles(T, topo, a)[3][r]))
        P.matmul_mx(T.ps[:, 512 * k:512 * k + C], T.vq[:], T.vs[:],
                    cod[:, c0:c0 + C], pla[:, c0:c0 + C], True, True).then_inc(S["y%d" % k], 1)
        p = 2 * C * h + C * (base // 2)
        src, dst = T.ps[:, 512 * k:512 * k + C], T.ysb[:, p:p + C]
        e = V if k == 3 else A
        e.wait_ge(S["y%d" % k], 1)
        (V.tensor_copy(dst, src) if e is V else A.activation(dst, src, Copy)).then_inc(S["c%d" % k], 1)
    for e in (V, A):
        e.wait_ge(S["k14"], 1)
        for k in range(N):
            e.wait_ge(S["c%d" % k], 1)
    for j in range(2):
        a = 256 * j
        V.tensor_copy(T.yo[:, a:a + 128], T.ysb[:].indirect(T.poff[:, a // 16:a // 16 + 8])).then_inc(S["yd%d" % j], 1)
        A.activation(T.yo[:, a + 128:a + 256], T.ysb[:].indirect(T.poff[:, a // 16 + 8:a // 16 + 16]), Copy).then_inc(S["yd%d" % j], 1)
        g.sync.wait_ge(S["yd%d" % j], 2)
        g.sync.dma_start(T.y[:, a:a + 256], T.yo[:, a:a + 256]).then_inc(S["st"], 16)
    g.sync.wait_ge(S["st"], 32)
    g.wait_ge(S["ls"], 2 * sum(len(hop1[q]) * len(runs[q]) for q in hop1) + 4 * sum(len(e) for e in hop2.values()))
